import numpy as np
import ml_dtypes

BF16 = ml_dtypes.bfloat16


def bf(x):
    return np.asarray(x, np.float32).astype(BF16)


def f32(x):
    return np.asarray(x, np.float32)


def f64(x):
    return np.asarray(x).astype(np.float64)


def striped(idx):
    return np.tile(idx.reshape(-1, 16).T, (8, 1))


S, K, M, N = 512, 256, 256, 256


def setup_inputs():
    return {"table": bf(np.random.standard_normal((K, S))), "w": bf(np.random.standard_normal((K, M)) / np.sqrt(K)), "b": f32(0.5 * np.random.standard_normal((M, 1))), "offs": striped(np.random.permutation(np.tile(np.arange(S), 2))[:N])}


def reference(table, w, b, offs):
    idx = offs[:16].T.reshape(-1)
    x = f64(table)[:, idx]
    y = f64(w).T @ x
    return y + f64(b)

@@ -1,0 +1,47 @@
+import concourse.mybir as mybir
+
+P = 128
+S, K, M, N = 512, 256, 256, 256
+K_BLOCKS = K // P
+M_BLOCKS = M // P
+FLOPS = 2 * K * M * N
+
+BF16, F32, U16 = mybir.dt.bfloat16, mybir.dt.float32, mybir.dt.uint16
+
+
+def tile_gather_matmul_kernel(tc, table, w, b, offs, out):
+    nc = tc.nc
+    with (
+        tc.tile_pool(name="held", bufs=1) as held,
+        tc.psum_pool(name="psum", bufs=1) as psum,
+    ):
+        offsets = held.tile([P, N // 16], U16, name="offsets")
+        nc.sync.dma_start(offsets[:], offs)
+
+        table_blocks = []
+        w_blocks = []
+        for k in range(K_BLOCKS):
+            table_k = held.tile([P, S], BF16, name="table%d" % k)
+            nc.sync.dma_start(table_k[:], table[k * P : (k + 1) * P, :])
+            table_blocks.append(table_k)
+            w_k = held.tile([P, M], BF16, name="w%d" % k)
+            nc.scalar.dma_start(w_k[:], w[k * P : (k + 1) * P, :])
+            w_blocks.append(w_k)
+
+        bias = held.tile([P, M_BLOCKS], F32, name="bias")
+        with nc.allow_non_contiguous_dma(reason="256 single float32 values, one to a partition"):
+            nc.scalar.dma_start(bias[:], b.rearrange("(a p) o -> p (a o)", p=P))
+
+        for m in range(M_BLOCKS):
+            bank = psum.tile([P, N], F32, name="bank%d" % m)
+            for k in range(K_BLOCKS):
+                nc.tensor.matmul(
+                    bank[:],
+                    w_blocks[k][:, m * P : (m + 1) * P],
+                    table_blocks[k][:].indirect(offsets[:]),
+                    start=(k == 0),
+                    stop=(k == K_BLOCKS - 1),
+                )
+            staged = held.tile([P, N], F32, name="staged%d" % m)
+            nc.vector.tensor_scalar(staged[:], bank[:], bias[:, m : m + 1], None, mybir.AluOpType.add)
+            nc.sync.dma_start(out[m * P : (m + 1) * P, :], staged[:])

@@ -5,6 +5,7 @@ S, K, M, N = 512, 256, 256, 256
 K_BLOCKS = K // P
 M_BLOCKS = M // P
 FLOPS = 2 * K * M * N
+ROW_START = 256
 
 BF16, F32, U16 = mybir.dt.bfloat16, mybir.dt.float32, mybir.dt.uint16
 
@@ -15,22 +16,22 @@ def tile_gather_matmul_kernel(tc, table, w, b, offs, out):
         tc.tile_pool(name="held", bufs=1) as held,
         tc.psum_pool(name="psum", bufs=1) as psum,
     ):
-        offsets = held.tile([P, N // 16], U16, name="offsets")
+        offsets = held.tile([P, N // 16], U16, name="offsets", align_bytes=ROW_START)
         nc.sync.dma_start(offsets[:], offs)
 
         table_blocks = []
         w_blocks = []
         for k in range(K_BLOCKS):
-            table_k = held.tile([P, S], BF16, name="table%d" % k)
+            table_k = held.tile([P, S], BF16, name="table%d" % k, align_bytes=ROW_START)
             nc.sync.dma_start(table_k[:], table[k * P : (k + 1) * P, :])
             table_blocks.append(table_k)
-            w_k = held.tile([P, M], BF16, name="w%d" % k)
+            w_k = held.tile([P, M], BF16, name="w%d" % k, align_bytes=ROW_START)
             nc.scalar.dma_start(w_k[:], w[k * P : (k + 1) * P, :])
             w_blocks.append(w_k)
 
-        bias = held.tile([P, M_BLOCKS], F32, name="bias")
+        bias = held.tile([P, M_BLOCKS, ROW_START // 4], F32, name="bias", align_bytes=ROW_START)
         with nc.allow_non_contiguous_dma(reason="256 single float32 values, one to a partition"):
-            nc.scalar.dma_start(bias[:], b.rearrange("(a p) o -> p (a o)", p=P))
+            nc.scalar.dma_start(bias[:, :, 0:1], b.rearrange("(a p) o -> p a o", p=P))
 
         for m in range(M_BLOCKS):
             bank = psum.tile([P, N], F32, name="bank%d" % m)
@@ -42,6 +43,6 @@ def tile_gather_matmul_kernel(tc, table, w, b, offs, out):
                     start=(k == 0),
                     stop=(k == K_BLOCKS - 1),
                 )
-            staged = held.tile([P, N], F32, name="staged%d" % m)
-            nc.vector.tensor_scalar(staged[:], bank[:], bias[:, m : m + 1], None, mybir.AluOpType.add)
+            staged = held.tile([P, N], F32, name="staged%d" % m, align_bytes=ROW_START)
+            nc.vector.tensor_scalar(staged[:], bank[:], bias[:, m, 0:1], None, mybir.AluOpType.add)
             nc.sync.dma_start(out[m * P : (m + 1) * P, :], staged[:])

@@ -20,14 +20,13 @@ def tile_gather_matmul_kernel(tc, table, w, b, offs, out):
         nc.sync.dma_start(offsets[:], offs)
 
         table_blocks = []
-        w_blocks = []
         for k in range(K_BLOCKS):
             table_k = held.tile([P, S], BF16, name="table%d" % k, align_bytes=ROW_START)
             nc.sync.dma_start(table_k[:], table[k * P : (k + 1) * P, :])
             table_blocks.append(table_k)
-            w_k = held.tile([P, M], BF16, name="w%d" % k, align_bytes=ROW_START)
-            nc.scalar.dma_start(w_k[:], w[k * P : (k + 1) * P, :])
-            w_blocks.append(w_k)
+
+        w_both = held.tile([P, K_BLOCKS, M], BF16, name="w_both", align_bytes=ROW_START)
+        nc.scalar.dma_start(w_both[:], w.rearrange("(k p) m -> p k m", p=P))
 
         bias = held.tile([P, M_BLOCKS, ROW_START // 4], F32, name="bias", align_bytes=ROW_START)
         with nc.allow_non_contiguous_dma(reason="256 single float32 values, one to a partition"):
@@ -38,7 +37,7 @@ def tile_gather_matmul_kernel(tc, table, w, b, offs, out):
             for k in range(K_BLOCKS):
                 nc.tensor.matmul(
                     bank[:],
-                    w_blocks[k][:, m * P : (m + 1) * P],
+                    w_both[:, k, m * P : (m + 1) * P],
                     table_blocks[k][:].indirect(offsets[:]),
                     start=(k == 0),
                     stop=(k == K_BLOCKS - 1),

import concourse.mybir as mybir

P = 128
S, K, M, N = 512, 256, 256, 256
K_BLOCKS = K // P
M_BLOCKS = M // P
FLOPS = 2 * K * M * N
ROW_START = 256

BF16, F32, U16 = mybir.dt.bfloat16, mybir.dt.float32, mybir.dt.uint16


def tile_gather_matmul_kernel(tc, table, w, b, offs, out):
    nc = tc.nc
    with (
        tc.tile_pool(name="held", bufs=1) as held,
        tc.psum_pool(name="psum", bufs=1) as psum,
    ):
        offsets = held.tile([P, N // 16], U16, name="offsets", align_bytes=ROW_START)
        nc.sync.dma_start(offsets[:], offs)

        table_blocks = []
        for k in range(K_BLOCKS):
            table_k = held.tile([P, S], BF16, name="table%d" % k, align_bytes=ROW_START)
            nc.sync.dma_start(table_k[:], table[k * P : (k + 1) * P, :])
            table_blocks.append(table_k)

        w_both = held.tile([P, K_BLOCKS, M], BF16, name="w_both", align_bytes=ROW_START)
        nc.scalar.dma_start(w_both[:], w.rearrange("(k p) m -> p k m", p=P))

        bias = held.tile([P, M_BLOCKS, ROW_START // 4], F32, name="bias", align_bytes=ROW_START)
        with nc.allow_non_contiguous_dma(reason="256 single float32 values, one to a partition"):
            nc.scalar.dma_start(bias[:, :, 0:1], b.rearrange("(a p) o -> p a o", p=P))

        for m in range(M_BLOCKS):
            bank = psum.tile([P, N], F32, name="bank%d" % m)
            for k in range(K_BLOCKS):
                nc.tensor.matmul(
                    bank[:],
                    w_both[:, k, m * P : (m + 1) * P],
                    table_blocks[k][:].indirect(offsets[:]),
                    start=(k == 0),
                    stop=(k == K_BLOCKS - 1),
                )
            staged = held.tile([P, N], F32, name="staged%d" % m, align_bytes=ROW_START)
            nc.vector.tensor_scalar(staged[:], bank[:], bias[:, m, 0:1], None, mybir.AluOpType.add)
            nc.sync.dma_start(out[m * P : (m + 1) * P, :], staged[:])
